import numpy as np
import ml_dtypes


def mxq(x, axis, fmt="e4m3"):
    dtype, down = {"e4m3": (ml_dtypes.float8_e4m3fn, 7), "e5m2": (ml_dtypes.float8_e5m2, 14)}[fmt]
    v = np.moveaxis(np.asarray(x, np.float32).astype(ml_dtypes.bfloat16).astype(np.float64), axis, -1)
    blocks = v.reshape(v.shape[:-1] + (-1, 32))
    amax = np.abs(blocks).max(-1, keepdims=True)
    byte = np.maximum(np.where(amax > 0, np.frexp(amax)[1] - 1 + 127, 0) - down, 1)
    scale = np.exp2(byte - 127.0)
    codes = (blocks / scale).astype(np.float32).astype(dtype).astype(np.float64)
    return np.moveaxis((codes * scale).reshape(v.shape), -1, axis)


WIDE = False


def mx_kscale(k):
    if not WIDE:
        return np.ones(k)
    levels = np.array([10, -10, 5, -5, 0])
    if k % 512:
        return np.exp2(np.random.permutation(np.resize(levels, k // 32))).repeat(32)
    a = np.empty((k // 512, 16))
    for p in range(k // 512):
        a[p, :8] = np.random.permutation(np.resize(levels, 8))
        for g in range(8):
            far = levels[np.abs(levels - a[p, g]) >= 10]
            a[p, g + 8] = far[np.random.randint(len(far))]
    return np.exp2(a.ravel()).repeat(32)


BF16 = ml_dtypes.bfloat16


def bf(x):
    return np.asarray(x, np.float32).astype(BF16)


def f64(x):
    return np.asarray(x).astype(np.float64)


E2M1 = np.array([0.0, 0.5, 1.0, 1.5, 2.0, 3.0, 4.0, 6.0, -0.0, -0.5, -1.0, -1.5, -2.0, -3.0, -4.0, -6.0])


def pack_weight(w, fmt):
    k, n = w.shape
    w = f64(bf(w)).reshape(k // 32, 32, n)
    amax = np.abs(w).max(1)
    if fmt == "e4m3":
        byte = np.frexp(amax)[1] - 1 + 127 - 7
    else:
        mant, ex = np.frexp(amax / 6.0)
        byte = np.where(mant > 0.5, ex, ex - 1) + 127
    byte = np.clip(np.where(amax > 0, byte, 1), 1, 254)
    scaled = (w * np.exp2(127.0 - byte)[:, None, :]).reshape(k, n).astype(np.float32)
    by_word = np.ascontiguousarray(scaled.reshape(k // 512, 128, 4, n).transpose(0, 1, 3, 2))
    if fmt == "e4m3":
        words = by_word.astype(ml_dtypes.float8_e4m3fn).view(np.uint8)
    else:
        c = by_word.astype(ml_dtypes.float4_e2m1fn).view(np.uint8) & 0xF
        words = c[..., 0::2] | (c[..., 1::2] << 4)
    return np.ascontiguousarray(words), np.ascontiguousarray(byte.astype(np.uint8).reshape(k // 512, 16, n))


def unpack_weight(words, scales, fmt):
    g, p, n, _ = words.shape
    if fmt == "e4m3":
        vals = np.ascontiguousarray(words).view(ml_dtypes.float8_e4m3fn).astype(np.float64)
    else:
        nib = np.empty((g, p, n, 4), np.uint8)
        nib[..., 0::2] = words & 0xF
        nib[..., 1::2] = words >> 4
        vals = E2M1[nib]
    vals = vals * np.repeat(np.exp2(scales.astype(np.float64) - 127.0), 8, axis=1)[..., None]
    return vals.transpose(0, 1, 3, 2).reshape(g * 512, n)
def pack4(w):
    words, scales = pack_weight(w, "e2m1")
    return words.reshape(words.shape[0], 128, -1), scales


def unpack4(words, scales):
    return unpack_weight(words.reshape(words.shape[0], 128, -1, 2), scales, "e2m1")


M, K, N = 768, 1536, 1024


def setup_inputs():
    s = mx_kscale(K)
    pools = []
    for _ in range(3):
        o = np.random.standard_normal((K, N)) / np.sqrt(K)
        lam = np.exp(0.3 * np.random.standard_normal((K // 2, 1)))
        turned = np.concatenate([lam * o[K // 2:], -lam * o[:K // 2]], axis=0)
        pools.append(turned / s[:, None])
    help_words, help_scales = pack4(pools[0])
    truth_words, truth_scales = pack_weight(pools[1], "e4m3")
    return {"v": bf(np.random.standard_normal((M, K)) * s),
            "help_words": help_words, "help_scales": help_scales,
            "truth_words": truth_words, "truth_scales": truth_scales,
            "safe": bf(pools[2])}


def reference(v, help_words, help_scales, truth_words, truth_scales, safe):
    vq = mxq(f64(v), 1, "e4m3")
    a = vq @ unpack4(help_words, help_scales)
    b = vq @ unpack_weight(truth_words, truth_scales, "e4m3")
    c = vq @ mxq(f64(safe), 0, "e4m3")
    z = np.minimum(a + b, c)
    return 1.0 / (1.0 + np.exp(-z))

@@ -1,0 +1,233 @@
+from contextlib import ExitStack
+
+import concourse.mybir as mybir
+from concourse.masks import make_identity
+
+M, K, N = 768, 1536, 1024
+FLOPS = 3 * 2 * M * K * N
+
+F32 = mybir.dt.float32
+BF16 = mybir.dt.bfloat16
+I32 = mybir.dt.int32
+U32 = mybir.dt.uint32
+U8 = mybir.dt.uint8
+FP8X4 = mybir.dt.float8_e4m3fn_x4
+FP4X4 = mybir.dt.float4_e2m1fn_x4
+SIGMOID = mybir.ActivationFunctionType.Sigmoid
+MIN = mybir.AluOpType.min
+
+P = 128
+K_PASS = 512
+GROUPS = K // K_PASS
+M_BLOCKS = M // P
+N_TILE = 512
+N_TILES = N // N_TILE
+
+
+def tile_skew_preference_min_s10_kernel(tc, v, help_words, help_scales, truth_words, truth_scales, safe, out):
+    nc = tc.nc
+    with ExitStack() as ctx:
+        keep = ctx.enter_context(tc.tile_pool(name="keep", bufs=1))
+        psum = ctx.enter_context(tc.psum_pool(name="psum", bufs=8))
+        ctx.enter_context(tc.manual_schedule())
+
+        identity = keep.tile([P, P], F32, name="identity", align_bytes=64)
+        help_planes = keep.tile([P, GROUPS * N], U8, name="help_planes", align_bytes=64)
+        truth_planes = keep.tile([P, GROUPS * N], U8, name="truth_planes", align_bytes=64)
+        warm = keep.tile([P, 2], F32, name="warm", align_bytes=64)
+
+        v_raw = []
+        for m in range(M_BLOCKS):
+            raw = keep.tile([P, K], BF16, name="v_raw%d" % m, align_bytes=64)
+            v_raw.append(raw)
+        v_grouped, v_codes, v_planes = [], [], []
+        banks_of_v = M_BLOCKS * GROUPS // 2
+        for b in range(banks_of_v):
+            grouped = keep.tile([P, 1024], BF16, name="v_grouped%d" % b, align_bytes=64)
+            codes = keep.tile([P, 256], U32, name="v_codes%d" % b, align_bytes=64)
+            planes = keep.tile([P, 256], U8, name="v_planes%d" % b, align_bytes=64)
+            v_grouped.append(grouped)
+            v_codes.append(codes)
+            v_planes.append(planes)
+        help_codes, truth_codes, safe_raw, safe_grouped, safe_codes, safe_planes = [], [], [], [], [], []
+        for g in range(GROUPS):
+            hc = keep.tile([P, 2 * N], U8, name="help_codes%d" % g, align_bytes=64)
+            tcodes = keep.tile([P, 4 * N], U8, name="truth_codes%d" % g, align_bytes=64)
+            sr = keep.tile([P, 4, N], BF16, name="safe_raw%d" % g, align_bytes=64)
+            help_codes.append(hc)
+            truth_codes.append(tcodes)
+            safe_raw.append(sr)
+            for n in range(N_TILES):
+                sg = keep.tile([P, N_TILE, 4], BF16, name="safe_grouped%d_%d" % (g, n), align_bytes=64)
+                sc = keep.tile([P, N_TILE], U32, name="safe_codes%d_%d" % (g, n), align_bytes=64)
+                sp = keep.tile([P, N_TILE], U8, name="safe_planes%d_%d" % (g, n), align_bytes=64)
+                safe_grouped.append(sg)
+                safe_codes.append(sc)
+                safe_planes.append(sp)
+
+        nc.vector.memset(help_planes[:].bitcast(I32), 0)
+        nc.vector.memset(warm[:], 0.0)
+        nc.vector.memset(truth_planes[:].bitcast(I32), 0)
+        make_identity(nc, identity[:])
+
+        def load_v(m):
+            nc.sync.dma_start(out=v_raw[m][:], in_=v[m * P : (m + 1) * P, :])
+
+        def load_planes(engine, planes, scales, first):
+            for q in range(4):
+                engine.dma_start(
+                    out=planes[32 * q + first : 32 * q + first + 4, :].bitcast(I32).rearrange("r (g n) -> r g n", g=GROUPS),
+                    in_=scales[:, 4 * q : 4 * q + 4, :].bitcast(I32).rearrange("g r n -> r g n"),
+                )
+
+        load_v(0)
+        load_v(1)
+        load_planes(nc.scalar, help_planes, help_scales, 0)
+        for m in range(2, M_BLOCKS):
+            load_v(m)
+        for g in range(GROUPS):
+            nc.sync.dma_start(out=help_codes[g][:].bitcast(I32), in_=help_words[g].bitcast(I32))
+        load_planes(nc.sync, truth_planes, truth_scales, 4)
+        for g in range(GROUPS):
+            nc.sync.dma_start(
+                out=truth_codes[g][:].bitcast(I32), in_=truth_words[g].rearrange("p n t -> p (n t)").bitcast(I32)
+            )
+        for g in range(GROUPS):
+            nc.sync.dma_start(
+                out=safe_raw[g][:], in_=safe[g * K_PASS : (g + 1) * K_PASS, :].rearrange("(p t) n -> p t n", t=4)
+            )
+
+        nc.scalar.activation(out=warm[:, 1:2], in_=warm[:, 0:1], func=SIGMOID)
+
+        def copy_v(b, bank):
+            source = bank[:].rearrange("p (q u r) -> p q r u", q=2, u=2)
+            target = v_grouped[b][:].bitcast(F32).rearrange("p (q r u) -> p q r u", q=2, u=2)
+            if b % 3 == 1:
+                nc.vector.tensor_copy(out=target, in_=source)
+            else:
+                nc.scalar.copy(out=target, in_=source)
+
+        def quantise_v(b):
+            nc.vector.quantize_mx(out=v_codes[b][:].bitcast(FP8X4), scales=v_planes[b][:], in_=v_grouped[b][:])
+
+        for b in range(banks_of_v):
+            bank = psum.tile([P, 512], F32, name="bank")
+            for q in range(2):
+                m, g = divmod(2 * b + q, GROUPS)
+                words = v_raw[m][:].bitcast(F32)
+                for u in range(2):
+                    at = (2 * q + u) * P
+                    nc.tensor.transpose(bank[:, at : at + P], words[:, 256 * g + u : 256 * (g + 1) : 2], identity[:])
+            copy_v(b, bank)
+            if b > 0:
+                quantise_v(b - 1)
+        quantise_v(banks_of_v - 1)
+
+        def interleave_safe(i):
+            g, n = divmod(i, N_TILES)
+            nc.vector.tensor_copy(
+                out=safe_grouped[i][:].rearrange("p (c i) t -> p c t i", i=4),
+                in_=safe_raw[g][:, :, n * N_TILE : (n + 1) * N_TILE].rearrange("p t (c i) -> p c t i", i=4),
+            )
+
+        def quantise_safe(i):
+            nc.vector.quantize_mx(
+                out=safe_codes[i][:].bitcast(FP8X4),
+                scales=safe_planes[i][:],
+                in_=safe_grouped[i][:].rearrange("p c t -> p (c t)"),
+            )
+
+        for i in range(GROUPS * N_TILES):
+            interleave_safe(i)
+            if i > 0:
+                quantise_safe(i - 1)
+        quantise_safe(GROUPS * N_TILES - 1)
+
+        def v_operand(m, g):
+            b, q = divmod(m * GROUPS + g, 2)
+            cols = slice(q * P, (q + 1) * P)
+            return v_codes[b][:, cols].bitcast(FP8X4), v_planes[b][:, cols]
+
+        def help_pass(acc, m, n, g):
+            lhsT, lhsT_scale = v_operand(m, g)
+            nc.tensor.matmul_mx(
+                out=acc[:],
+                lhsT=lhsT,
+                lhsT_scale=lhsT_scale,
+                rhs=help_codes[g][:, n * 1024 : (n + 1) * 1024].bitcast(FP4X4),
+                rhs_scale=help_planes[:, g * N + n * N_TILE : g * N + (n + 1) * N_TILE],
+                start=(g == 0),
+                stop=False,
+            )
+
+        def truth_pass(acc, m, n, g):
+            lhsT, lhsT_scale = v_operand(m, g)
+            nc.tensor.matmul_mx(
+                out=acc[:],
+                lhsT=lhsT,
+                lhsT_scale=lhsT_scale,
+                rhs=truth_codes[g][:, n * 2048 : (n + 1) * 2048].bitcast(FP8X4),
+                rhs_scale=truth_planes[4:P, g * N + n * N_TILE : g * N + (n + 1) * N_TILE],
+                start=False,
+                stop=(g == GROUPS - 1),
+            )
+
+        def safe_pass(acc, m, n, g, cols):
+            lhsT, lhsT_scale = v_operand(m, g)
+            nc.tensor.matmul_mx(
+                out=acc,
+                lhsT=lhsT,
+                lhsT_scale=lhsT_scale,
+                rhs=safe_codes[g * N_TILES + n][:, cols].bitcast(FP8X4),
+                rhs_scale=safe_planes[g * N_TILES + n][:, cols],
+                start=(g == 0),
+                stop=(g == GROUPS - 1),
+            )
+
+        tiles = []
+        for m in range(M_BLOCKS):
+            for n in range(N_TILES):
+                tiles.append((m, n))
+
+        sums = []
+
+        def copy_sum(i, acc):
+            kept = keep.tile([P, N_TILE], F32, name="sum%d" % i, align_bytes=64)
+            nc.scalar.copy(out=kept[:], in_=acc[:])
+            sums.append(kept)
+
+        first = tiles[:6]
+        accs = []
+        for m, n in first:
+            acc = psum.tile([P, 512], F32, name="bank")
+            accs.append(acc)
+        for g in range(GROUPS):
+            for i, (m, n) in enumerate(first):
+                help_pass(accs[i], m, n, g)
+        for i, (m, n) in enumerate(first):
+            for g in range(GROUPS):
+                truth_pass(accs[i], m, n, g)
+            copy_sum(i, accs[i])
+        for i in range(6, 12):
+            m, n = tiles[i]
+            acc = psum.tile([P, 512], F32, name="bank")
+            for g in range(GROUPS):
+                help_pass(acc, m, n, g)
+            for g in range(GROUPS):
+                truth_pass(acc, m, n, g)
+            copy_sum(i, acc)
+
+        for i, (m, n) in enumerate(tiles):
+            low = keep.tile([P, N_TILE], F32, name="low%d" % i, align_bytes=64)
+            res = keep.tile([P, N_TILE], F32, name="res%d" % i, align_bytes=64)
+            width = N_TILE if i < 11 else 256
+            for at in range(0, N_TILE, width):
+                cols = slice(at, at + width)
+                acc = psum.tile([P, 512], F32, name="bank")
+                for g in range(GROUPS):
+                    safe_pass(acc[:, 0:width], m, n, g, cols)
+                nc.vector.tensor_tensor(out=low[:, cols], in0=acc[:, 0:width], in1=sums[i][:, cols], op=MIN)
+                nc.scalar.activation(out=res[:, cols], in_=low[:, cols], func=SIGMOID)
+                nc.sync.dma_start(
+                    out=out[m * P : (m + 1) * P, n * N_TILE + at : n * N_TILE + at + width], in_=res[:, cols]
+                )

@@ -22,6 +22,10 @@ GROUPS = K // K_PASS
 M_BLOCKS = M // P
 N_TILE = 512
 N_TILES = N // N_TILE
+BY_TENSOR = (0, 1, 2)
+BY_VECTOR = (3, 4, 5)
+BANKS_ON_VECTOR = (1, 4)
+LAST_WIDTHS = (256, 128, 128)
 
 
 def tile_skew_preference_min_s10_kernel(tc, v, help_words, help_scales, truth_words, truth_scales, safe, out):
@@ -31,67 +35,70 @@ def tile_skew_preference_min_s10_kernel(tc, v, help_words, help_scales, truth_wo
         psum = ctx.enter_context(tc.psum_pool(name="psum", bufs=8))
         ctx.enter_context(tc.manual_schedule())
 
-        identity = keep.tile([P, P], F32, name="identity", align_bytes=64)
-        help_planes = keep.tile([P, GROUPS * N], U8, name="help_planes", align_bytes=64)
-        truth_planes = keep.tile([P, GROUPS * N], U8, name="truth_planes", align_bytes=64)
-        warm = keep.tile([P, 2], F32, name="warm", align_bytes=64)
+        def sbuf(shape, dtype, name):
+            tile = keep.tile(shape, dtype, name=name, align_bytes=64)
+            return tile
 
-        v_raw = []
-        for m in range(M_BLOCKS):
-            raw = keep.tile([P, K], BF16, name="v_raw%d" % m, align_bytes=64)
-            v_raw.append(raw)
-        v_grouped, v_codes, v_planes = [], [], []
-        banks_of_v = M_BLOCKS * GROUPS // 2
-        for b in range(banks_of_v):
-            grouped = keep.tile([P, 1024], BF16, name="v_grouped%d" % b, align_bytes=64)
-            codes = keep.tile([P, 256], U32, name="v_codes%d" % b, align_bytes=64)
-            planes = keep.tile([P, 256], U8, name="v_planes%d" % b, align_bytes=64)
-            v_grouped.append(grouped)
-            v_codes.append(codes)
-            v_planes.append(planes)
-        help_codes, truth_codes, safe_raw, safe_grouped, safe_codes, safe_planes = [], [], [], [], [], []
-        for g in range(GROUPS):
-            hc = keep.tile([P, 2 * N], U8, name="help_codes%d" % g, align_bytes=64)
-            tcodes = keep.tile([P, 4 * N], U8, name="truth_codes%d" % g, align_bytes=64)
-            sr = keep.tile([P, 4, N], BF16, name="safe_raw%d" % g, align_bytes=64)
-            help_codes.append(hc)
-            truth_codes.append(tcodes)
-            safe_raw.append(sr)
-            for n in range(N_TILES):
-                sg = keep.tile([P, N_TILE, 4], BF16, name="safe_grouped%d_%d" % (g, n), align_bytes=64)
-                sc = keep.tile([P, N_TILE], U32, name="safe_codes%d_%d" % (g, n), align_bytes=64)
-                sp = keep.tile([P, N_TILE], U8, name="safe_planes%d_%d" % (g, n), align_bytes=64)
-                safe_grouped.append(sg)
-                safe_codes.append(sc)
-                safe_planes.append(sp)
+        identity = sbuf([P, P], F32, "identity")
+        warm = sbuf([P, 2], F32, "warm")
+        help_planes = sbuf([P, GROUPS, N], U8, "help_planes")
+        truth_planes = sbuf([P, GROUPS, N], U8, "truth_planes")
+        help_codes = sbuf([P, GROUPS, 2 * N], U8, "help_codes")
+        truth_codes = [sbuf([P, 4 * N], U8, "truth_codes%d" % g) for g in range(GROUPS)]
+        v_raw = [sbuf([P, K], BF16, "v_raw%d" % m) for m in range(M_BLOCKS)]
+        v_grouped = [sbuf([P, GROUPS * P * 4], BF16, "v_grouped%d" % m) for m in range(M_BLOCKS)]
+        v_codes = [sbuf([P, GROUPS * P], U32, "v_codes%d" % m) for m in range(M_BLOCKS)]
+        v_planes = [sbuf([P, GROUPS * P], U8, "v_planes%d" % m) for m in range(M_BLOCKS)]
+        v_sorted = {m: sbuf([P, K // 2], F32, "v_sorted%d" % m) for m in BY_VECTOR}
+        v_turned = {m: sbuf([P, K // 2], F32, "v_turned%d" % m) for m in BY_VECTOR}
+        safe_raw = [sbuf([P, 4, N], BF16, "safe_raw%d" % g) for g in range(GROUPS)]
+        safe_grouped = [sbuf([P, N, 4], BF16, "safe_grouped%d" % g) for g in range(GROUPS)]
+        safe_codes = [sbuf([P, N], U32, "safe_codes%d" % g) for g in range(GROUPS)]
+        safe_planes = [sbuf([P, N], U8, "safe_planes%d" % g) for g in range(GROUPS)]
 
-        nc.vector.memset(help_planes[:].bitcast(I32), 0)
+        nc.vector.memset(help_planes[:].rearrange("p g n -> p (g n)").bitcast(I32), 0)
         nc.vector.memset(warm[:], 0.0)
-        nc.vector.memset(truth_planes[:].bitcast(I32), 0)
+        nc.vector.memset(truth_planes[:].rearrange("p g n -> p (g n)").bitcast(I32), 0)
         make_identity(nc, identity[:])
 
-        def load_v(m):
-            nc.sync.dma_start(out=v_raw[m][:], in_=v[m * P : (m + 1) * P, :])
+        def load_v(m, cols):
+            nc.sync.dma_start(out=v_raw[m][:, cols], in_=v[m * P : (m + 1) * P, cols])
+
+        def load_v_quarters(m):
+            source = v[m * P : (m + 1) * P, :].rearrange("(j s) (g x) -> j (s g) x", s=4, g=GROUPS)
+            for a in (0, 2, 1, 3):
+                nc.sync.dma_start(
+                    out=v_raw[m][32 * a : 32 * a + 32, :].rearrange("j (b x) -> j b x", x=P),
+                    in_=source[:, :, a * P : (a + 1) * P],
+                )
 
         def load_planes(engine, planes, scales, first):
             for q in range(4):
                 engine.dma_start(
-                    out=planes[32 * q + first : 32 * q + first + 4, :].bitcast(I32).rearrange("r (g n) -> r g n", g=GROUPS),
+                    out=planes[32 * q + first : 32 * q + first + 4, :, :].bitcast(I32),
                     in_=scales[:, 4 * q : 4 * q + 4, :].bitcast(I32).rearrange("g r n -> r g n"),
                 )
 
-        load_v(0)
-        load_v(1)
+        def load_help(first, last):
+            nc.sync.dma_start(
+                out=help_codes[:, first:last, :].bitcast(I32),
+                in_=help_words[first:last].rearrange("g p b -> p g b").bitcast(I32),
+            )
+
+        load_v(0, slice(0, K))
+        load_v(1, slice(0, K))
         load_planes(nc.scalar, help_planes, help_scales, 0)
-        for m in range(2, M_BLOCKS):
-            load_v(m)
-        for g in range(GROUPS):
-            nc.sync.dma_start(out=help_codes[g][:].bitcast(I32), in_=help_words[g].bitcast(I32))
+        load_v(2, slice(0, 2 * K_PASS))
+        load_v(2, slice(2 * K_PASS, K))
+        load_help(0, 1)
+        load_help(1, 3)
         load_planes(nc.sync, truth_planes, truth_scales, 4)
         for g in range(GROUPS):
             nc.sync.dma_start(
                 out=truth_codes[g][:].bitcast(I32), in_=truth_words[g].rearrange("p n t -> p (n t)").bitcast(I32)
             )
+        for m in BY_VECTOR:
+            load_v_quarters(m)
         for g in range(GROUPS):
             nc.sync.dma_start(
                 out=safe_raw[g][:], in_=safe[g * K_PASS : (g + 1) * K_PASS, :].rearrange("(p t) n -> p t n", t=4)
@@ -99,135 +106,166 @@ def tile_skew_preference_min_s10_kernel(tc, v, help_words, help_scales, truth_wo
 
         nc.scalar.activation(out=warm[:, 1:2], in_=warm[:, 0:1], func=SIGMOID)
 
-        def copy_v(b, bank):
-            source = bank[:].rearrange("p (q u r) -> p q r u", q=2, u=2)
-            target = v_grouped[b][:].bitcast(F32).rearrange("p (q r u) -> p q r u", q=2, u=2)
-            if b % 3 == 1:
-                nc.vector.tensor_copy(out=target, in_=source)
-            else:
-                nc.scalar.copy(out=target, in_=source)
-
-        def quantise_v(b):
-            nc.vector.quantize_mx(out=v_codes[b][:].bitcast(FP8X4), scales=v_planes[b][:], in_=v_grouped[b][:])
-
-        for b in range(banks_of_v):
-            bank = psum.tile([P, 512], F32, name="bank")
-            for q in range(2):
-                m, g = divmod(2 * b + q, GROUPS)
-                words = v_raw[m][:].bitcast(F32)
-                for u in range(2):
-                    at = (2 * q + u) * P
-                    nc.tensor.transpose(bank[:, at : at + P], words[:, 256 * g + u : 256 * (g + 1) : 2], identity[:])
-            copy_v(b, bank)
-            if b > 0:
-                quantise_v(b - 1)
-        quantise_v(banks_of_v - 1)
-
-        def interleave_safe(i):
-            g, n = divmod(i, N_TILES)
-            nc.vector.tensor_copy(
-                out=safe_grouped[i][:].rearrange("p (c i) t -> p c t i", i=4),
-                in_=safe_raw[g][:, :, n * N_TILE : (n + 1) * N_TILE].rearrange("p t (c i) -> p c t i", i=4),
-            )
-
-        def quantise_safe(i):
+        def quantise_v(m, first, last):
             nc.vector.quantize_mx(
-                out=safe_codes[i][:].bitcast(FP8X4),
-                scales=safe_planes[i][:],
-                in_=safe_grouped[i][:].rearrange("p c t -> p (c t)"),
+                out=v_codes[m][:, first * P : last * P].bitcast(FP8X4),
+                scales=v_planes[m][:, first * P : last * P],
+                in_=v_grouped[m][:, first * K_PASS : last * K_PASS],
             )
 
-        for i in range(GROUPS * N_TILES):
-            interleave_safe(i)
-            if i > 0:
-                quantise_safe(i - 1)
-        quantise_safe(GROUPS * N_TILES - 1)
+        def turn_on_tensor(blocks):
+            units = [(m, g) for m in blocks for g in range(GROUPS)]
+            waiting = []
+            for b in range((len(units) + 1) // 2):
+                bank = psum.tile([P, 512], F32, name="bank")
+                here = units[2 * b : 2 * b + 2]
+                for q, (m, g) in enumerate(here):
+                    words = v_raw[m][:].bitcast(F32)
+                    for u in range(2):
+                        at = (2 * q + u) * P
+                        nc.tensor.transpose(bank[:, at : at + P], words[:, 256 * g + u : 256 * (g + 1) : 2], identity[:])
+                for q, (m, g) in enumerate(here):
+                    source = bank[:, 256 * q : 256 * (q + 1)].rearrange("p (u r) -> p r u", u=2)
+                    target = v_grouped[m][:, g * K_PASS : (g + 1) * K_PASS].bitcast(F32).rearrange("p (r u) -> p r u", u=2)
+                    if b in BANKS_ON_VECTOR:
+                        nc.vector.tensor_copy(out=target, in_=source)
+                    else:
+                        nc.scalar.copy(out=target, in_=source)
+                for m, g in waiting:
+                    quantise_v(m, g, g + 1)
+                waiting = here
+            for m, g in waiting:
+                quantise_v(m, g, g + 1)
 
-        def v_operand(m, g):
-            b, q = divmod(m * GROUPS + g, 2)
-            cols = slice(q * P, (q + 1) * P)
-            return v_codes[b][:, cols].bitcast(FP8X4), v_planes[b][:, cols]
+        def turn_on_vector(m):
+            for g in range(GROUPS):
+                nc.vector.tensor_copy(
+                    out=v_sorted[m][:, 256 * g : 256 * (g + 1)].rearrange("p (s u i) -> p s u i", s=4, u=2),
+                    in_=v_raw[m][:].bitcast(F32).rearrange("p (s g i u) -> p g s u i", s=4, g=GROUPS, u=2)[:, g],
+                )
+            for g in range(GROUPS):
+                nc.vector.transpose(
+                    out=v_turned[m][:, 256 * g : 256 * (g + 1)], in_=v_sorted[m][:, 256 * g : 256 * (g + 1)]
+                )
+            for g in range(GROUPS):
+                nc.vector.tensor_copy(
+                    out=v_grouped[m][:, g * K_PASS : (g + 1) * K_PASS]
+                    .bitcast(F32)
+                    .rearrange("p (j h w) -> p h j w", h=2, w=4),
+                    in_=v_turned[m][:, 256 * g : 256 * (g + 1)].rearrange("p (h w j) -> p h j w", h=2, w=4),
+                )
+            quantise_v(m, 0, 2)
+            quantise_v(m, 2, 3)
 
-        def help_pass(acc, m, n, g):
-            lhsT, lhsT_scale = v_operand(m, g)
-            nc.tensor.matmul_mx(
-                out=acc[:],
-                lhsT=lhsT,
-                lhsT_scale=lhsT_scale,
-                rhs=help_codes[g][:, n * 1024 : (n + 1) * 1024].bitcast(FP4X4),
-                rhs_scale=help_planes[:, g * N + n * N_TILE : g * N + (n + 1) * N_TILE],
-                start=(g == 0),
-                stop=False,
+        def interleave_safe(copy, g, first, last):
+            copy(
+                out=safe_grouped[g][:, first:last, :].rearrange("p (c i) t -> p c t i", i=4),
+                in_=safe_raw[g][:, :, first:last].rearrange("p t (c i) -> p c t i", i=4),
             )
 
-        def truth_pass(acc, m, n, g):
-            lhsT, lhsT_scale = v_operand(m, g)
-            nc.tensor.matmul_mx(
-                out=acc[:],
-                lhsT=lhsT,
-                lhsT_scale=lhsT_scale,
-                rhs=truth_codes[g][:, n * 2048 : (n + 1) * 2048].bitcast(FP8X4),
-                rhs_scale=truth_planes[4:P, g * N + n * N_TILE : g * N + (n + 1) * N_TILE],
-                start=False,
-                stop=(g == GROUPS - 1),
+        def quantise_safe(g, n):
+            cols = slice(n * N_TILE, (n + 1) * N_TILE)
+            nc.vector.quantize_mx(
+                out=safe_codes[g][:, cols].bitcast(FP8X4),
+                scales=safe_planes[g][:, cols],
+                in_=safe_grouped[g][:, cols, :].rearrange("p c t -> p (c t)"),
             )
 
-        def safe_pass(acc, m, n, g, cols):
-            lhsT, lhsT_scale = v_operand(m, g)
+        def prepare_safe(g):
+            split = 512 if g < 2 else 768
+            interleave_safe(nc.vector.tensor_copy, g, 0, 512)
+            interleave_safe(nc.scalar.copy, g, split, N)
+            if split > 512:
+                interleave_safe(nc.vector.tensor_copy, g, 512, split)
+            quantise_safe(g, 0)
+            quantise_safe(g, 1)
+
+        def mx_pass(acc, m, g, rhs, rhs_scale, start, stop):
+            cols = slice(g * P, (g + 1) * P)
             nc.tensor.matmul_mx(
                 out=acc,
-                lhsT=lhsT,
-                lhsT_scale=lhsT_scale,
-                rhs=safe_codes[g * N_TILES + n][:, cols].bitcast(FP8X4),
-                rhs_scale=safe_planes[g * N_TILES + n][:, cols],
-                start=(g == 0),
-                stop=(g == GROUPS - 1),
+                lhsT=v_codes[m][:, cols].bitcast(FP8X4),
+                lhsT_scale=v_planes[m][:, cols],
+                rhs=rhs,
+                rhs_scale=rhs_scale,
+                start=start,
+                stop=stop,
             )
 
-        tiles = []
-        for m in range(M_BLOCKS):
-            for n in range(N_TILES):
-                tiles.append((m, n))
+        def help_pass(acc, m, n, g):
+            codes = help_codes[:, g, n * 1024 : (n + 1) * 1024].bitcast(FP4X4)
+            planes = help_planes[:, g, n * N_TILE : (n + 1) * N_TILE]
+            mx_pass(acc[:], m, g, codes, planes, g == 0, False)
 
-        sums = []
+        def truth_pass(acc, m, n, g):
+            codes = truth_codes[g][:, n * 2048 : (n + 1) * 2048].bitcast(FP8X4)
+            planes = truth_planes[4:P, g, n * N_TILE : (n + 1) * N_TILE]
+            mx_pass(acc[:], m, g, codes, planes, False, g == GROUPS - 1)
 
-        def copy_sum(i, acc):
-            kept = keep.tile([P, N_TILE], F32, name="sum%d" % i, align_bytes=64)
-            nc.scalar.copy(out=kept[:], in_=acc[:])
-            sums.append(kept)
+        def safe_pass(acc, m, g, first, width):
+            cols = slice(first, first + width)
+            mx_pass(acc[:, 0:width], m, g, safe_codes[g][:, cols].bitcast(FP8X4), safe_planes[g][:, cols], g == 0, g == GROUPS - 1)
 
-        first = tiles[:6]
-        accs = []
-        for m, n in first:
-            acc = psum.tile([P, 512], F32, name="bank")
-            accs.append(acc)
+        open_banks = {}
+        sums = {}
+
+        def help_blocks(blocks):
+            tiles = [(m, n) for m in blocks for n in range(N_TILES)]
+            for tile in tiles:
+                bank = psum.tile([P, 512], F32, name="bank")
+                open_banks[tile] = bank
+            for g in range(GROUPS):
+                for m, n in tiles:
+                    help_pass(open_banks[(m, n)], m, n, g)
+
+        def truth_blocks(blocks):
+            for m in blocks:
+                for n in range(N_TILES):
+                    for g in range(GROUPS):
+                        truth_pass(open_banks[(m, n)], m, n, g)
+                    kept = sbuf([P, N_TILE], F32, "sum%d_%d" % (m, n))
+                    nc.scalar.copy(out=kept[:], in_=open_banks[(m, n)][:])
+                    sums[(m, n)] = kept
+
+        def finish(bank, m, n, first, width):
+            low = sbuf([P, width], F32, "low%d_%d_%d" % (m, n, first))
+            result = sbuf([P, width], F32, "result%d_%d_%d" % (m, n, first))
+            nc.vector.tensor_tensor(out=low[:], in0=bank[:, 0:width], in1=sums[(m, n)][:, first : first + width], op=MIN)
+            nc.scalar.activation(out=result[:], in_=low[:], func=SIGMOID)
+            at = n * N_TILE + first
+            nc.sync.dma_start(out=out[m * P : (m + 1) * P, at : at + width], in_=result[:])
+
+        turn_on_tensor(BY_TENSOR)
+        help_blocks(BY_TENSOR)
+        turn_on_vector(3)
+        truth_blocks(BY_TENSOR)
+        turn_on_vector(4)
+        help_blocks((3,))
+        truth_blocks((3,))
+        turn_on_vector(5)
+        prepare_safe(0)
+        help_blocks((4,))
+        truth_blocks((4,))
+        prepare_safe(1)
+        help_blocks((5,))
+        truth_blocks((5,))
+        prepare_safe(2)
+
+        early = [(m, n) for m in BY_TENSOR for n in range(N_TILES)]
+        for tile in early:
+            bank = psum.tile([P, 512], F32, name="bank")
+            open_banks[tile] = bank
         for g in range(GROUPS):
-            for i, (m, n) in enumerate(first):
-                help_pass(accs[i], m, n, g)
-        for i, (m, n) in enumerate(first):
-            for g in range(GROUPS):
-                truth_pass(accs[i], m, n, g)
-            copy_sum(i, accs[i])
-        for i in range(6, 12):
-            m, n = tiles[i]
-            acc = psum.tile([P, 512], F32, name="bank")
-            for g in range(GROUPS):
-                help_pass(acc, m, n, g)
-            for g in range(GROUPS):
-                truth_pass(acc, m, n, g)
-            copy_sum(i, acc)
-
-        for i, (m, n) in enumerate(tiles):
-            low = keep.tile([P, N_TILE], F32, name="low%d" % i, align_bytes=64)
-            res = keep.tile([P, N_TILE], F32, name="res%d" % i, align_bytes=64)
-            width = N_TILE if i < 11 else 256
-            for at in range(0, N_TILE, width):
-                cols = slice(at, at + width)
-                acc = psum.tile([P, 512], F32, name="bank")
-                for g in range(GROUPS):
-                    safe_pass(acc[:, 0:width], m, n, g, cols)
-                nc.vector.tensor_tensor(out=low[:, cols], in0=acc[:, 0:width], in1=sums[i][:, cols], op=MIN)
-                nc.scalar.activation(out=res[:, cols], in_=low[:, cols], func=SIGMOID)
-                nc.sync.dma_start(
-                    out=out[m * P : (m + 1) * P, n * N_TILE + at : n * N_TILE + at + width], in_=res[:, cols]
-                )
+            for m, n in early:
+                safe_pass(open_banks[(m, n)], m, g, n * N_TILE, N_TILE)
+                if g == GROUPS - 1:
+                    finish(open_banks[(m, n)], m, n, 0, N_TILE)
+        for m in BY_VECTOR:
+            for n in range(N_TILES):
+                first = 0
+                for width in LAST_WIDTHS if (m, n) == (M_BLOCKS - 1, N_TILES - 1) else (N_TILE,):
+                    bank = psum.tile([P, 512], F32, name="bank")
+                    for g in range(GROUPS):
+                        safe_pass(bank, m, g, n * N_TILE + first, width)
+                    finish(bank, m, n, first, width)
+                    first = first + width

@@ -25,6 +25,11 @@ N_TILES = N // N_TILE
 BY_TENSOR = (0, 1, 2)
 BY_VECTOR = (3, 4, 5)
 BANKS_ON_VECTOR = (1, 4)
+SAFE_SPLIT = (512, 512, 640)
+IDLE_PASSES = 16
+MOVING_CODES_AT = 64
+STATIONARY_CODES_AT = 192
+STATIONARY_PLANES_AT = 128
 LAST_WIDTHS = (256, 128, 128)
 
 
@@ -36,26 +41,36 @@ def tile_skew_preference_min_s10_kernel(tc, v, help_words, help_scales, truth_wo
         ctx.enter_context(tc.manual_schedule())
 
         def sbuf(shape, dtype, name):
-            tile = keep.tile(shape, dtype, name=name, align_bytes=64)
+            tile = keep.tile(shape, dtype, name=name, align_bytes=256)
             return tile
+
+        def shifted(width, dtype, name, at):
+            size = 1 if dtype == U8 else 4
+            tile = sbuf([P, at // size + width], dtype, name)
+            return tile[:, at // size :]
 
         identity = sbuf([P, P], F32, "identity")
         warm = sbuf([P, 2], F32, "warm")
         help_planes = sbuf([P, GROUPS, N], U8, "help_planes")
         truth_planes = sbuf([P, GROUPS, N], U8, "truth_planes")
-        help_codes = sbuf([P, GROUPS, 2 * N], U8, "help_codes")
-        truth_codes = [sbuf([P, 4 * N], U8, "truth_codes%d" % g) for g in range(GROUPS)]
+        help_codes = shifted(GROUPS * 2 * N, U8, "help_codes", MOVING_CODES_AT)
+        truth_codes = [shifted(4 * N, U8, "truth_codes%d" % g, MOVING_CODES_AT) for g in range(GROUPS)]
         v_raw = [sbuf([P, K], BF16, "v_raw%d" % m) for m in range(M_BLOCKS)]
         v_grouped = [sbuf([P, GROUPS * P * 4], BF16, "v_grouped%d" % m) for m in range(M_BLOCKS)]
-        v_codes = [sbuf([P, GROUPS * P], U32, "v_codes%d" % m) for m in range(M_BLOCKS)]
-        v_planes = [sbuf([P, GROUPS * P], U8, "v_planes%d" % m) for m in range(M_BLOCKS)]
+        v_codes = [shifted(GROUPS * P, U32, "v_codes%d" % m, STATIONARY_CODES_AT) for m in range(M_BLOCKS)]
+        v_planes = [shifted(GROUPS * P, U8, "v_planes%d" % m, STATIONARY_PLANES_AT) for m in range(M_BLOCKS)]
         v_sorted = {m: sbuf([P, K // 2], F32, "v_sorted%d" % m) for m in BY_VECTOR}
         v_turned = {m: sbuf([P, K // 2], F32, "v_turned%d" % m) for m in BY_VECTOR}
+        idle = sbuf([P, K_PASS], BF16, "idle")
+        idle_codes = sbuf([P, P], U32, "idle_codes")
+        idle_planes = sbuf([P, P], U8, "idle_planes")
         safe_raw = [sbuf([P, 4, N], BF16, "safe_raw%d" % g) for g in range(GROUPS)]
         safe_grouped = [sbuf([P, N, 4], BF16, "safe_grouped%d" % g) for g in range(GROUPS)]
-        safe_codes = [sbuf([P, N], U32, "safe_codes%d" % g) for g in range(GROUPS)]
+        safe_codes = [shifted(N, U32, "safe_codes%d" % g, MOVING_CODES_AT) for g in range(GROUPS)]
         safe_planes = [sbuf([P, N], U8, "safe_planes%d" % g) for g in range(GROUPS)]
 
+        nc.gpsimd.memset(idle[:], 0.0)
+        nc.vector.quantize_mx(out=idle_codes[:].bitcast(FP8X4), scales=idle_planes[:], in_=idle[:])
         nc.vector.memset(help_planes[:].rearrange("p g n -> p (g n)").bitcast(I32), 0)
         nc.vector.memset(warm[:], 0.0)
         nc.vector.memset(truth_planes[:].rearrange("p g n -> p (g n)").bitcast(I32), 0)
@@ -81,21 +96,20 @@ def tile_skew_preference_min_s10_kernel(tc, v, help_words, help_scales, truth_wo
 
         def load_help(first, last):
             nc.sync.dma_start(
-                out=help_codes[:, first:last, :].bitcast(I32),
+                out=help_codes[:, first * 2 * N : last * 2 * N].bitcast(I32).rearrange("p (g b) -> p g b", g=last - first),
                 in_=help_words[first:last].rearrange("g p b -> p g b").bitcast(I32),
             )
 
         load_v(0, slice(0, K))
         load_v(1, slice(0, K))
         load_planes(nc.scalar, help_planes, help_scales, 0)
-        load_v(2, slice(0, 2 * K_PASS))
-        load_v(2, slice(2 * K_PASS, K))
+        load_v(2, slice(0, K))
         load_help(0, 1)
         load_help(1, 3)
         load_planes(nc.sync, truth_planes, truth_scales, 4)
         for g in range(GROUPS):
             nc.sync.dma_start(
-                out=truth_codes[g][:].bitcast(I32), in_=truth_words[g].rearrange("p n t -> p (n t)").bitcast(I32)
+                out=truth_codes[g].bitcast(I32), in_=truth_words[g].rearrange("p n t -> p (n t)").bitcast(I32)
             )
         for m in BY_VECTOR:
             load_v_quarters(m)
@@ -172,7 +186,7 @@ def tile_skew_preference_min_s10_kernel(tc, v, help_words, help_scales, truth_wo
             )
 
         def prepare_safe(g):
-            split = 512 if g < 2 else 768
+            split = SAFE_SPLIT[g]
             interleave_safe(nc.vector.tensor_copy, g, 0, 512)
             interleave_safe(nc.scalar.copy, g, split, N)
             if split > 512:
@@ -193,7 +207,8 @@ def tile_skew_preference_min_s10_kernel(tc, v, help_words, help_scales, truth_wo
             )
 
         def help_pass(acc, m, n, g):
-            codes = help_codes[:, g, n * 1024 : (n + 1) * 1024].bitcast(FP4X4)
+            first = g * 2 * N + n * 1024
+            codes = help_codes[:, first : first + 1024].bitcast(FP4X4)
             planes = help_planes[:, g, n * N_TILE : (n + 1) * N_TILE]
             mx_pass(acc[:], m, g, codes, planes, g == 0, False)
 
@@ -228,12 +243,24 @@ def tile_skew_preference_min_s10_kernel(tc, v, help_words, help_scales, truth_wo
                     sums[(m, n)] = kept
 
         def finish(bank, m, n, first, width):
-            low = sbuf([P, width], F32, "low%d_%d_%d" % (m, n, first))
+            low = sums[(m, n)][:, first : first + width]
             result = sbuf([P, width], F32, "result%d_%d_%d" % (m, n, first))
-            nc.vector.tensor_tensor(out=low[:], in0=bank[:, 0:width], in1=sums[(m, n)][:, first : first + width], op=MIN)
-            nc.scalar.activation(out=result[:], in_=low[:], func=SIGMOID)
+            nc.vector.tensor_tensor(out=low, in0=bank[:, 0:width], in1=low, op=MIN)
+            nc.scalar.activation(out=result[:], in_=low, func=SIGMOID)
             at = n * N_TILE + first
             nc.sync.dma_start(out=out[m * P : (m + 1) * P, at : at + width], in_=result[:])
+
+        idle_bank = psum.tile([P, 512], F32, name="bank")
+        for i in range(IDLE_PASSES):
+            nc.tensor.matmul_mx(
+                out=idle_bank[:, 0:P],
+                lhsT=idle_codes[:].bitcast(FP8X4),
+                lhsT_scale=idle_planes[:],
+                rhs=idle_codes[:].bitcast(FP8X4),
+                rhs_scale=idle_planes[:],
+                start=True,
+                stop=True,
+            )
 
         turn_on_tensor(BY_TENSOR)
         help_blocks(BY_TENSOR)

from contextlib import ExitStack

import concourse.mybir as mybir
from concourse.masks import make_identity

M, K, N = 768, 1536, 1024
FLOPS = 3 * 2 * M * K * N

F32 = mybir.dt.float32
BF16 = mybir.dt.bfloat16
I32 = mybir.dt.int32
U32 = mybir.dt.uint32
U8 = mybir.dt.uint8
FP8X4 = mybir.dt.float8_e4m3fn_x4
FP4X4 = mybir.dt.float4_e2m1fn_x4
SIGMOID = mybir.ActivationFunctionType.Sigmoid
MIN = mybir.AluOpType.min

P = 128
K_PASS = 512
GROUPS = K // K_PASS
M_BLOCKS = M // P
N_TILE = 512
N_TILES = N // N_TILE
BY_TENSOR = (0, 1, 2)
BY_VECTOR = (3, 4, 5)
BANKS_ON_VECTOR = (1, 4)
SAFE_SPLIT = (512, 512, 640)
IDLE_PASSES = 16
MOVING_CODES_AT = 64
STATIONARY_CODES_AT = 192
STATIONARY_PLANES_AT = 128
LAST_WIDTHS = (256, 128, 128)


def tile_skew_preference_min_s10_kernel(tc, v, help_words, help_scales, truth_words, truth_scales, safe, out):
    nc = tc.nc
    with ExitStack() as ctx:
        keep = ctx.enter_context(tc.tile_pool(name="keep", bufs=1))
        psum = ctx.enter_context(tc.psum_pool(name="psum", bufs=8))
        ctx.enter_context(tc.manual_schedule())

        def sbuf(shape, dtype, name):
            tile = keep.tile(shape, dtype, name=name, align_bytes=256)
            return tile

        def shifted(width, dtype, name, at):
            size = 1 if dtype == U8 else 4
            tile = sbuf([P, at // size + width], dtype, name)
            return tile[:, at // size :]

        identity = sbuf([P, P], F32, "identity")
        warm = sbuf([P, 2], F32, "warm")
        help_planes = sbuf([P, GROUPS, N], U8, "help_planes")
        truth_planes = sbuf([P, GROUPS, N], U8, "truth_planes")
        help_codes = shifted(GROUPS * 2 * N, U8, "help_codes", MOVING_CODES_AT)
        truth_codes = [shifted(4 * N, U8, "truth_codes%d" % g, MOVING_CODES_AT) for g in range(GROUPS)]
        v_raw = [sbuf([P, K], BF16, "v_raw%d" % m) for m in range(M_BLOCKS)]
        v_grouped = [sbuf([P, GROUPS * P * 4], BF16, "v_grouped%d" % m) for m in range(M_BLOCKS)]
        v_codes = [shifted(GROUPS * P, U32, "v_codes%d" % m, STATIONARY_CODES_AT) for m in range(M_BLOCKS)]
        v_planes = [shifted(GROUPS * P, U8, "v_planes%d" % m, STATIONARY_PLANES_AT) for m in range(M_BLOCKS)]
        v_sorted = {m: sbuf([P, K // 2], F32, "v_sorted%d" % m) for m in BY_VECTOR}
        v_turned = {m: sbuf([P, K // 2], F32, "v_turned%d" % m) for m in BY_VECTOR}
        idle = sbuf([P, K_PASS], BF16, "idle")
        idle_codes = sbuf([P, P], U32, "idle_codes")
        idle_planes = sbuf([P, P], U8, "idle_planes")
        safe_raw = [sbuf([P, 4, N], BF16, "safe_raw%d" % g) for g in range(GROUPS)]
        safe_grouped = [sbuf([P, N, 4], BF16, "safe_grouped%d" % g) for g in range(GROUPS)]
        safe_codes = [shifted(N, U32, "safe_codes%d" % g, MOVING_CODES_AT) for g in range(GROUPS)]
        safe_planes = [sbuf([P, N], U8, "safe_planes%d" % g) for g in range(GROUPS)]

        nc.gpsimd.memset(idle[:], 0.0)
        nc.vector.quantize_mx(out=idle_codes[:].bitcast(FP8X4), scales=idle_planes[:], in_=idle[:])
        nc.vector.memset(help_planes[:].rearrange("p g n -> p (g n)").bitcast(I32), 0)
        nc.vector.memset(warm[:], 0.0)
        nc.vector.memset(truth_planes[:].rearrange("p g n -> p (g n)").bitcast(I32), 0)
        make_identity(nc, identity[:])

        def load_v(m, cols):
            nc.sync.dma_start(out=v_raw[m][:, cols], in_=v[m * P : (m + 1) * P, cols])

        def load_v_quarters(m):
            source = v[m * P : (m + 1) * P, :].rearrange("(j s) (g x) -> j (s g) x", s=4, g=GROUPS)
            for a in (0, 2, 1, 3):
                nc.sync.dma_start(
                    out=v_raw[m][32 * a : 32 * a + 32, :].rearrange("j (b x) -> j b x", x=P),
                    in_=source[:, :, a * P : (a + 1) * P],
                )

        def load_planes(engine, planes, scales, first):
            for q in range(4):
                engine.dma_start(
                    out=planes[32 * q + first : 32 * q + first + 4, :, :].bitcast(I32),
                    in_=scales[:, 4 * q : 4 * q + 4, :].bitcast(I32).rearrange("g r n -> r g n"),
                )

        def load_help(first, last):
            nc.sync.dma_start(
                out=help_codes[:, first * 2 * N : last * 2 * N].bitcast(I32).rearrange("p (g b) -> p g b", g=last - first),
                in_=help_words[first:last].rearrange("g p b -> p g b").bitcast(I32),
            )

        load_v(0, slice(0, K))
        load_v(1, slice(0, K))
        load_planes(nc.scalar, help_planes, help_scales, 0)
        load_v(2, slice(0, K))
        load_help(0, 1)
        load_help(1, 3)
        load_planes(nc.sync, truth_planes, truth_scales, 4)
        for g in range(GROUPS):
            nc.sync.dma_start(
                out=truth_codes[g].bitcast(I32), in_=truth_words[g].rearrange("p n t -> p (n t)").bitcast(I32)
            )
        for m in BY_VECTOR:
            load_v_quarters(m)
        for g in range(GROUPS):
            nc.sync.dma_start(
                out=safe_raw[g][:], in_=safe[g * K_PASS : (g + 1) * K_PASS, :].rearrange("(p t) n -> p t n", t=4)
            )

        nc.scalar.activation(out=warm[:, 1:2], in_=warm[:, 0:1], func=SIGMOID)

        def quantise_v(m, first, last):
            nc.vector.quantize_mx(
                out=v_codes[m][:, first * P : last * P].bitcast(FP8X4),
                scales=v_planes[m][:, first * P : last * P],
                in_=v_grouped[m][:, first * K_PASS : last * K_PASS],
            )

        def turn_on_tensor(blocks):
            units = [(m, g) for m in blocks for g in range(GROUPS)]
            waiting = []
            for b in range((len(units) + 1) // 2):
                bank = psum.tile([P, 512], F32, name="bank")
                here = units[2 * b : 2 * b + 2]
                for q, (m, g) in enumerate(here):
                    words = v_raw[m][:].bitcast(F32)
                    for u in range(2):
                        at = (2 * q + u) * P
                        nc.tensor.transpose(bank[:, at : at + P], words[:, 256 * g + u : 256 * (g + 1) : 2], identity[:])
                for q, (m, g) in enumerate(here):
                    source = bank[:, 256 * q : 256 * (q + 1)].rearrange("p (u r) -> p r u", u=2)
                    target = v_grouped[m][:, g * K_PASS : (g + 1) * K_PASS].bitcast(F32).rearrange("p (r u) -> p r u", u=2)
                    if b in BANKS_ON_VECTOR:
                        nc.vector.tensor_copy(out=target, in_=source)
                    else:
                        nc.scalar.copy(out=target, in_=source)
                for m, g in waiting:
                    quantise_v(m, g, g + 1)
                waiting = here
            for m, g in waiting:
                quantise_v(m, g, g + 1)

        def turn_on_vector(m):
            for g in range(GROUPS):
                nc.vector.tensor_copy(
                    out=v_sorted[m][:, 256 * g : 256 * (g + 1)].rearrange("p (s u i) -> p s u i", s=4, u=2),
                    in_=v_raw[m][:].bitcast(F32).rearrange("p (s g i u) -> p g s u i", s=4, g=GROUPS, u=2)[:, g],
                )
            for g in range(GROUPS):
                nc.vector.transpose(
                    out=v_turned[m][:, 256 * g : 256 * (g + 1)], in_=v_sorted[m][:, 256 * g : 256 * (g + 1)]
                )
            for g in range(GROUPS):
                nc.vector.tensor_copy(
                    out=v_grouped[m][:, g * K_PASS : (g + 1) * K_PASS]
                    .bitcast(F32)
                    .rearrange("p (j h w) -> p h j w", h=2, w=4),
                    in_=v_turned[m][:, 256 * g : 256 * (g + 1)].rearrange("p (h w j) -> p h j w", h=2, w=4),
                )
            quantise_v(m, 0, 2)
            quantise_v(m, 2, 3)

        def interleave_safe(copy, g, first, last):
            copy(
                out=safe_grouped[g][:, first:last, :].rearrange("p (c i) t -> p c t i", i=4),
                in_=safe_raw[g][:, :, first:last].rearrange("p t (c i) -> p c t i", i=4),
            )

        def quantise_safe(g, n):
            cols = slice(n * N_TILE, (n + 1) * N_TILE)
            nc.vector.quantize_mx(
                out=safe_codes[g][:, cols].bitcast(FP8X4),
                scales=safe_planes[g][:, cols],
                in_=safe_grouped[g][:, cols, :].rearrange("p c t -> p (c t)"),
            )

        def prepare_safe(g):
            split = SAFE_SPLIT[g]
            interleave_safe(nc.vector.tensor_copy, g, 0, 512)
            interleave_safe(nc.scalar.copy, g, split, N)
            if split > 512:
                interleave_safe(nc.vector.tensor_copy, g, 512, split)
            quantise_safe(g, 0)
            quantise_safe(g, 1)

        def mx_pass(acc, m, g, rhs, rhs_scale, start, stop):
            cols = slice(g * P, (g + 1) * P)
            nc.tensor.matmul_mx(
                out=acc,
                lhsT=v_codes[m][:, cols].bitcast(FP8X4),
                lhsT_scale=v_planes[m][:, cols],
                rhs=rhs,
                rhs_scale=rhs_scale,
                start=start,
                stop=stop,
            )

        def help_pass(acc, m, n, g):
            first = g * 2 * N + n * 1024
            codes = help_codes[:, first : first + 1024].bitcast(FP4X4)
            planes = help_planes[:, g, n * N_TILE : (n + 1) * N_TILE]
            mx_pass(acc[:], m, g, codes, planes, g == 0, False)

        def truth_pass(acc, m, n, g):
            codes = truth_codes[g][:, n * 2048 : (n + 1) * 2048].bitcast(FP8X4)
            planes = truth_planes[4:P, g, n * N_TILE : (n + 1) * N_TILE]
            mx_pass(acc[:], m, g, codes, planes, False, g == GROUPS - 1)

        def safe_pass(acc, m, g, first, width):
            cols = slice(first, first + width)
            mx_pass(acc[:, 0:width], m, g, safe_codes[g][:, cols].bitcast(FP8X4), safe_planes[g][:, cols], g == 0, g == GROUPS - 1)

        open_banks = {}
        sums = {}

        def help_blocks(blocks):
            tiles = [(m, n) for m in blocks for n in range(N_TILES)]
            for tile in tiles:
                bank = psum.tile([P, 512], F32, name="bank")
                open_banks[tile] = bank
            for g in range(GROUPS):
                for m, n in tiles:
                    help_pass(open_banks[(m, n)], m, n, g)

        def truth_blocks(blocks):
            for m in blocks:
                for n in range(N_TILES):
                    for g in range(GROUPS):
                        truth_pass(open_banks[(m, n)], m, n, g)
                    kept = sbuf([P, N_TILE], F32, "sum%d_%d" % (m, n))
                    nc.scalar.copy(out=kept[:], in_=open_banks[(m, n)][:])
                    sums[(m, n)] = kept

        def finish(bank, m, n, first, width):
            low = sums[(m, n)][:, first : first + width]
            result = sbuf([P, width], F32, "result%d_%d_%d" % (m, n, first))
            nc.vector.tensor_tensor(out=low, in0=bank[:, 0:width], in1=low, op=MIN)
            nc.scalar.activation(out=result[:], in_=low, func=SIGMOID)
            at = n * N_TILE + first
            nc.sync.dma_start(out=out[m * P : (m + 1) * P, at : at + width], in_=result[:])

        idle_bank = psum.tile([P, 512], F32, name="bank")
        for i in range(IDLE_PASSES):
            nc.tensor.matmul_mx(
                out=idle_bank[:, 0:P],
                lhsT=idle_codes[:].bitcast(FP8X4),
                lhsT_scale=idle_planes[:],
                rhs=idle_codes[:].bitcast(FP8X4),
                rhs_scale=idle_planes[:],
                start=True,
                stop=True,
            )

        turn_on_tensor(BY_TENSOR)
        help_blocks(BY_TENSOR)
        turn_on_vector(3)
        truth_blocks(BY_TENSOR)
        turn_on_vector(4)
        help_blocks((3,))
        truth_blocks((3,))
        turn_on_vector(5)
        prepare_safe(0)
        help_blocks((4,))
        truth_blocks((4,))
        prepare_safe(1)
        help_blocks((5,))
        truth_blocks((5,))
        prepare_safe(2)

        early = [(m, n) for m in BY_TENSOR for n in range(N_TILES)]
        for tile in early:
            bank = psum.tile([P, 512], F32, name="bank")
            open_banks[tile] = bank
        for g in range(GROUPS):
            for m, n in early:
                safe_pass(open_banks[(m, n)], m, g, n * N_TILE, N_TILE)
                if g == GROUPS - 1:
                    finish(open_banks[(m, n)], m, n, 0, N_TILE)
        for m in BY_VECTOR:
            for n in range(N_TILES):
                first = 0
                for width in LAST_WIDTHS if (m, n) == (M_BLOCKS - 1, N_TILES - 1) else (N_TILE,):
                    bank = psum.tile([P, 512], F32, name="bank")
                    for g in range(GROUPS):
                        safe_pass(bank, m, g, n * N_TILE + first, width)
                    finish(bank, m, n, first, width)
                    first = first + width
